import numpy as np
import ml_dtypes


def mxq(x, axis, fmt="e4m3"):
    dtype, down = {"e4m3": (ml_dtypes.float8_e4m3fn, 7), "e5m2": (ml_dtypes.float8_e5m2, 14)}[fmt]
    v = np.moveaxis(np.asarray(x, np.float32).astype(ml_dtypes.bfloat16).astype(np.float64), axis, -1)
    blocks = v.reshape(v.shape[:-1] + (-1, 32))
    amax = np.abs(blocks).max(-1, keepdims=True)
    byte = np.maximum(np.where(amax > 0, np.frexp(amax)[1] - 1 + 127, 0) - down, 1)
    scale = np.exp2(byte - 127.0)
    codes = (blocks / scale).astype(np.float32).astype(dtype).astype(np.float64)
    return np.moveaxis((codes * scale).reshape(v.shape), -1, axis)


WIDE = False


def mx_kscale(k):
    if not WIDE:
        return np.ones(k)
    levels = np.array([10, -10, 5, -5, 0])
    if k % 512:
        return np.exp2(np.random.permutation(np.resize(levels, k // 32))).repeat(32)
    a = np.empty((k // 512, 16))
    for p in range(k // 512):
        a[p, :8] = np.random.permutation(np.resize(levels, 8))
        for g in range(8):
            far = levels[np.abs(levels - a[p, g]) >= 10]
            a[p, g + 8] = far[np.random.randint(len(far))]
    return np.exp2(a.ravel()).repeat(32)


def f64(x):
    return np.asarray(x).astype(np.float64)


def striped(idx):
    return np.tile(idx.reshape(-1, 16).T, (8, 1)).astype(np.uint16)


def unstriped(offs):
    return offs[:16].T.reshape(-1).astype(np.int64)


def pack_weight(w):
    k, n = w.shape
    w = f64(np.asarray(w, np.float32).astype(ml_dtypes.bfloat16)).reshape(k // 32, 32, n)
    amax = np.abs(w).max(1)
    byte = np.clip(np.where(amax > 0, np.frexp(amax)[1] - 1 + 127 - 7, 1), 1, 254)
    scaled = (w * np.exp2(127.0 - byte)[:, None, :]).reshape(k, n).astype(np.float32)
    words = np.ascontiguousarray(scaled.reshape(k // 512, 128, 4, n).transpose(0, 1, 3, 2)).astype(ml_dtypes.float8_e4m3fn).view(np.uint8)
    return words, np.ascontiguousarray(byte.astype(np.uint8).reshape(k // 512, 16, n))


def unpack_weight(words, scales):
    g, p, n, _ = words.shape
    vals = np.ascontiguousarray(words).view(ml_dtypes.float8_e4m3fn).astype(np.float64) * np.repeat(np.exp2(scales.astype(np.float64) - 127.0), 8, axis=1)[..., None]
    return vals.transpose(0, 1, 3, 2).reshape(g * 512, n)


def relu(v):
    return np.maximum(v, 0.0)


K, T, S, N, U = 512, 1024, 256, 256, 512


def setup_inputs():
    n = np.random.standard_normal
    s = mx_kscale(K)[:, None]
    packed_xT = pack_weight(n((K, T)) * s)
    return {
        "x_words": packed_xT[0],
        "x_scales": packed_xT[1],
        "w1": (n((K, N)) / np.sqrt(K) / s).astype(np.float32),
        "w2": (n((K, N)) / np.sqrt(K) / s).astype(np.float32),
        "bot": (0.5 * n((N, S))).astype(np.float32),
        "offs": striped(np.random.permutation(T)[:S]),
        "lf": striped(np.random.permutation(np.concatenate([np.arange(S), np.random.randint(0, S, U - S)]))),
        "rt": striped(np.random.permutation(np.concatenate([np.arange(S), np.random.randint(0, S, U - S)]))),
    }


def reference(x_words, x_scales, w1, w2, bot, offs, lf, rt):
    xq = unpack_weight(x_words, x_scales)[:, unstriped(offs)]
    yh = mxq(f64(w1), 0, "e4m3").T @ xq
    hh = 0.8 * (np.log(np.exp(yh) + 1.0))
    eta = hh + f64(bot)
    bm = np.maximum(f64(bot)[:, unstriped(lf)], f64(bot)[:, unstriped(rt)])
    hl = relu(eta[:, unstriped(lf)] - bm)
    yv = mxq(f64(w2), 0, "e4m3").T @ xq
    vl = yv[:, unstriped(lf)]
    hr = relu(eta[:, unstriped(rt)] - bm)
    vr = yv[:, unstriped(rt)]
    spd = np.maximum(np.abs(vl) + np.sqrt(hl + 0.01), np.abs(vr) + np.sqrt(hr + 0.01))
    return 0.5 * (hl * vl + hr * vr - (spd * (hr - hl)))

@@ -1,0 +1,171 @@
+from contextlib import ExitStack
+
+import concourse.mybir as mybir
+
+K, T, S, N, U = 512, 1024, 256, 256, 512
+FLOPS = 2 * 2 * K * N * S
+
+F32 = mybir.dt.float32
+BF16 = mybir.dt.bfloat16
+I32 = mybir.dt.int32
+U32 = mybir.dt.uint32
+U16 = mybir.dt.uint16
+U8 = mybir.dt.uint8
+FP8X4 = mybir.dt.float8_e4m3fn_x4
+ACT = mybir.ActivationFunctionType
+ALU = mybir.AluOpType
+
+P = 128
+PACK = 4
+BLOCKS = N // P
+WIDE = 2 * U
+COPY_WINDOW = 704
+
+
+def tile_picked_yshwat_mass_p_kernel(
+    tc, x_words, x_scales, w1, w2, bot, offs, lf, rt, out
+):
+    nc = tc.nc
+    with ExitStack() as ctx:
+        keep = ctx.enter_context(tc.tile_pool(name="keep", bufs=1))
+        psum = ctx.enter_context(tc.psum_pool(name="psum", bufs=1))
+
+        offs_t = keep.tile([P, S // 16], U16, name="offs_t")
+        lf_t = keep.tile([P, U // 16], U16, name="lf_t")
+        rt_t = keep.tile([P, U // 16], U16, name="rt_t")
+        sides = (lf_t, rt_t)
+        words = keep.tile([P, T], I32, name="words")
+        scales = keep.tile([P, T], U8, name="scales")
+        bot_w = [keep.tile([P, WIDE], F32, name=f"bot_w{b}") for b in range(BLOCKS)]
+        soft_w = [keep.tile([P, WIDE], F32, name=f"soft_w{b}") for b in range(BLOCKS)]
+        raw_h = keep.tile([P, PACK, N], F32, name="raw_h")
+        raw_v = keep.tile([P, PACK, N], F32, name="raw_v")
+
+        nc.gpsimd.memset(scales[:].bitcast(I32), 0)
+        nc.sync.dma_start(rt_t[:], rt)
+        nc.sync.dma_start(
+            bot_w[0][:, 0 : BLOCKS * S].rearrange("p (b s) -> p b s", b=BLOCKS),
+            bot.rearrange("(b p) s -> p b s", p=P),
+        )
+        nc.sync.dma_start(lf_t[:], lf)
+        nc.sync.dma_start(raw_v[:], w2.rearrange("(p j) n -> p j n", j=PACK))
+        for q in range(4):
+            nc.sync.dma_start(
+                scales[32 * q : 32 * q + 4, :].bitcast(I32),
+                x_scales[0, 4 * q : 4 * q + 4, :].bitcast(I32),
+            )
+        nc.sync.dma_start(offs_t[:], offs)
+        nc.sync.dma_start(words[:], x_words[0].rearrange("p n t -> p (n t)").bitcast(I32))
+        nc.sync.dma_start(raw_h[:], w1.rearrange("(p j) n -> p j n", j=PACK))
+        nc.scalar.copy(bot_w[1][:, 0:S], bot_w[0][:, S : 2 * S])
+
+        grouped_v = keep.tile([P, N, PACK], BF16, name="grouped_v", align_bytes=64)
+        grouped_h = keep.tile([P, N, PACK], BF16, name="grouped_h", align_bytes=64)
+        for grouped, raw in ((grouped_v, raw_v), (grouped_h, raw_h)):
+            nc.scalar.copy(
+                grouped[:].rearrange("p (c i) t -> p c t i", i=4),
+                raw[:].rearrange("p t (c i) -> p c t i", i=4),
+            )
+
+        bot_r = [keep.tile([P, U], F32, name=f"bot_r{b}") for b in range(BLOCKS)]
+        step0 = keep.tile([P, U], F32, name="step0")
+        nc.vector.tensor_copy(bot_r[0][:], bot_w[0][:].indirect(rt_t[:]))
+        nc.vector.tensor_tensor(step0[:], bot_w[0][:].indirect(lf_t[:]), bot_r[0][:], ALU.subtract)
+        nc.vector.tensor_copy(bot_r[1][:], bot_w[1][:].indirect(rt_t[:]))
+
+        x_codes = keep.tile([P, S], U32, name="x_codes", align_bytes=64)
+        x_sc = keep.tile([P, S], U8, name="x_sc", align_bytes=64)
+        nc.vector.tensor_copy(x_codes[:], words[:].bitcast(U32).indirect(offs_t[:]))
+        nc.vector.tensor_copy(x_sc[:], scales[:].indirect(offs_t[:]))
+
+        def product(grouped, name):
+            codes = keep.tile([P, N], U32, name=name + "_codes", align_bytes=64)
+            plane = keep.tile([P, N], U8, name=name + "_plane", align_bytes=64)
+            acc = psum.tile([P, BLOCKS, S], F32, name=name)
+            nc.vector.quantize_mx(
+                out=codes[:].bitcast(FP8X4), scales=plane[:], in_=grouped[:].rearrange("p n t -> p (n t)")
+            )
+            for b in range(BLOCKS):
+                cols = slice(b * P, (b + 1) * P)
+                nc.tensor.matmul_mx(
+                    out=acc[:, b, :],
+                    lhsT=codes[:, cols].bitcast(FP8X4),
+                    lhsT_scale=plane[:, cols],
+                    rhs=x_codes[:].bitcast(FP8X4),
+                    rhs_scale=x_sc[:],
+                    start=True,
+                    stop=True,
+                )
+            return acc
+
+        yv = product(grouped_v, "yv")
+        yh = product(grouped_h, "yh")
+
+        late = keep.tile([P, 5, U], F32, name="late", tag="grouped_h", align_bytes=64)
+        step = [step0[:], late[:, 4, :]]
+        vel = [late[:, 0:2, :], late[:, 2:4, :]]
+        nc.vector.tensor_tensor(step[1], bot_w[1][:].indirect(lf_t[:]), bot_r[1][:], ALU.subtract)
+
+        def cut_depths(b, tag):
+            cut = keep.tile([P, 2, U], F32, name=f"cut{b}", tag=tag)
+            nc.scalar.activation(cut[:, 0, :], step[b], ACT.Relu, scale=-1.25)
+            nc.scalar.activation(cut[:, 1, :], step[b], ACT.Relu, scale=1.25)
+            return cut
+
+        cut = [cut_depths(0, "raw_v")]
+        vel_w = keep.tile([P, S + COPY_WINDOW], F32, name="vel_w", tag="raw_h")
+        for b in range(BLOCKS):
+            nc.scalar.copy(vel_w[:, b * S : (b + 1) * S], yv[:, b, :])
+        size = keep.tile([P, BLOCKS * S], F32, name="size")
+        decay = keep.tile([P, BLOCKS * S], F32, name="decay")
+        tail = keep.tile([P, BLOCKS, S], F32, name="tail")
+        nc.scalar.activation(size[:], yh[:].rearrange("p b s -> p (b s)"), ACT.Abs)
+        nc.scalar.activation(decay[:], size[:], ACT.Exp, scale=-1.0)
+        nc.scalar.activation(tail[:].rearrange("p b s -> p (b s)"), decay[:], ACT.Ln, bias=1.0)
+        cut.append(cut_depths(1, "size"))
+
+        for b in range(BLOCKS):
+            for side in range(2):
+                nc.vector.tensor_copy(vel[b][:, side, :], vel_w[:, b * S : b * S + COPY_WINDOW].indirect(sides[side][:]))
+        for b in range(BLOCKS):
+            nc.vector.scalar_tensor_tensor(soft_w[b][:, 0:S], yh[:, b, :], 0.0, tail[:, b, :], ALU.max, ALU.add)
+
+        level = [keep.tile([P, 2, U], F32, name=f"level{b}") for b in range(BLOCKS)]
+        depth = [keep.tile([P, 2, U], F32, name=f"depth{b}") for b in range(BLOCKS)]
+        root = [keep.tile([P, 2, U], F32, name=f"root{b}") for b in range(BLOCKS)]
+        speed = []
+        for b, tag in enumerate(("decay", "level0")):
+            speed.append(keep.tile([P, 2, U], F32, name=f"speed{b}", tag=tag))
+            if b == 0:
+                nc.scalar.activation(speed[b][:], vel[b], ACT.Abs)
+            for side in range(2):
+                nc.vector.tensor_tensor(
+                    level[b][:, side, :], soft_w[b][:].indirect(sides[side][:]), cut[b][:, side, :], ALU.subtract
+                )
+            if b == 1:
+                nc.scalar.activation(speed[b][:], vel[b], ACT.Abs)
+            for side in range(2):
+                nc.scalar.activation(depth[b][:, side, :], level[b][:, side, :], ACT.Relu, scale=0.8)
+                nc.scalar.activation(root[b][:, side, :], depth[b][:, side, :], ACT.Sqrt, bias=0.01)
+
+        halves = [slice(0, U // 2), slice(U // 2, U)]
+        for b in range(BLOCKS):
+            wave = keep.tile([P, 2, U], F32, name=f"wave{b}")
+            fastest = keep.tile([P, U], F32, name=f"fastest{b}")
+            shifted = keep.tile([P, 2, U], F32, name=f"shifted{b}")
+            flux = keep.tile([P, 2, U], F32, name=f"flux{b}")
+            result = keep.tile([P, U], F32, name=f"result{b}")
+            for side in range(2):
+                nc.vector.tensor_tensor(wave[:, side, :], speed[b][:, side, :], root[b][:, side, :], ALU.add)
+            for c in halves:
+                nc.vector.tensor_tensor(fastest[:, c], wave[:, 0, c], wave[:, 1, c], ALU.max)
+            for c in halves:
+                nc.vector.tensor_tensor(shifted[:, 0, c], vel[b][:, 0, c], fastest[:, c], ALU.add)
+                nc.vector.tensor_tensor(shifted[:, 1, c], vel[b][:, 1, c], fastest[:, c], ALU.subtract)
+            for c in halves:
+                nc.vector.scalar_tensor_tensor(
+                    flux[:, :, c], depth[b][:, :, c], 0.5, shifted[:, :, c], ALU.mult, ALU.mult
+                )
+            for c in halves:
+                nc.vector.tensor_tensor(result[:, c], flux[:, 0, c], flux[:, 1, c], ALU.add)
+                nc.sync.dma_start(out[b * P : (b + 1) * P, c], result[:, c])

@@ -1,6 +1,7 @@
 from contextlib import ExitStack
 
 import concourse.mybir as mybir
+from concourse.masks import make_identity
 
 K, T, S, N, U = 512, 1024, 256, 256, 512
 FLOPS = 2 * 2 * K * N * S
@@ -42,6 +43,8 @@ def tile_picked_yshwat_mass_p_kernel(
         raw_v = keep.tile([P, PACK, N], F32, name="raw_v")
 
         nc.gpsimd.memset(scales[:].bitcast(I32), 0)
+        identity = keep.tile([P, P], F32, name="identity")
+        make_identity(nc, identity[:])
         nc.sync.dma_start(rt_t[:], rt)
         nc.sync.dma_start(
             bot_w[0][:, 0 : BLOCKS * S].rearrange("p (b s) -> p b s", b=BLOCKS),
@@ -115,18 +118,37 @@ def tile_picked_yshwat_mass_p_kernel(
         cut = [cut_depths(0, "raw_v")]
         vel_w = keep.tile([P, S + COPY_WINDOW], F32, name="vel_w", tag="raw_h")
         for b in range(BLOCKS):
-            nc.scalar.copy(vel_w[:, b * S : (b + 1) * S], yv[:, b, :])
+            nc.scalar.activation(vel_w[:, b * S : (b + 1) * S], yv[:, b, :], ACT.Copy, scale=0.4)
         size = keep.tile([P, BLOCKS * S], F32, name="size")
         decay = keep.tile([P, BLOCKS * S], F32, name="decay")
         tail = keep.tile([P, BLOCKS, S], F32, name="tail")
         nc.scalar.activation(size[:], yh[:].rearrange("p b s -> p (b s)"), ACT.Abs)
         nc.scalar.activation(decay[:], size[:], ACT.Exp, scale=-1.0)
         nc.scalar.activation(tail[:].rearrange("p b s -> p (b s)"), decay[:], ACT.Ln, bias=1.0)
+        warm = keep.tile([P, 1], F32, name="warm")
+        nc.scalar.activation(warm[:], tail[:, 0, 0:1], ACT.Sqrt, bias=1.0)
         cut.append(cut_depths(1, "size"))
 
-        for b in range(BLOCKS):
+        def turn(bank, tile, chunks, start, stop):
+            for n, c in enumerate(chunks):
+                nc.tensor.matmul(
+                    bank[:, n * P : (n + 1) * P],
+                    tile[:, c * P : (c + 1) * P],
+                    identity[:],
+                    start=start and n == 0,
+                    stop=stop and n == len(chunks) - 1,
+                    is_transpose=True,
+                )
+
+        every = range(U // P)
+        vel_turned = []
+        for b, tag in enumerate(("bank_a", "yv")):
             for side in range(2):
-                nc.vector.tensor_copy(vel[b][:, side, :], vel_w[:, b * S : b * S + COPY_WINDOW].indirect(sides[side][:]))
+                nc.vector.tensor_copy(
+                    vel[b][:, side, :], vel_w[:, b * S : b * S + COPY_WINDOW].indirect(sides[side][:])
+                )
+            vel_turned.append(psum.tile([P, U], F32, name=f"vel_turned{b}", tag=tag))
+            turn(vel_turned[b], vel[b][:, 0, :], every, True, True)
         for b in range(BLOCKS):
             nc.vector.scalar_tensor_tensor(soft_w[b][:, 0:S], yh[:, b, :], 0.0, tail[:, b, :], ALU.max, ALU.add)
 
@@ -134,38 +156,47 @@ def tile_picked_yshwat_mass_p_kernel(
         depth = [keep.tile([P, 2, U], F32, name=f"depth{b}") for b in range(BLOCKS)]
         root = [keep.tile([P, 2, U], F32, name=f"root{b}") for b in range(BLOCKS)]
         speed = []
-        for b, tag in enumerate(("decay", "level0")):
-            speed.append(keep.tile([P, 2, U], F32, name=f"speed{b}", tag=tag))
-            if b == 0:
-                nc.scalar.activation(speed[b][:], vel[b], ACT.Abs)
+        wave_l = []
+        for b, (tag, wave_tag) in enumerate((("decay", "bank_a"), ("level0", "yh"))):
             for side in range(2):
                 nc.vector.tensor_tensor(
                     level[b][:, side, :], soft_w[b][:].indirect(sides[side][:]), cut[b][:, side, :], ALU.subtract
                 )
-            if b == 1:
-                nc.scalar.activation(speed[b][:], vel[b], ACT.Abs)
-            for side in range(2):
-                nc.scalar.activation(depth[b][:, side, :], level[b][:, side, :], ACT.Relu, scale=0.8)
-                nc.scalar.activation(root[b][:, side, :], depth[b][:, side, :], ACT.Sqrt, bias=0.01)
+            level_turned = psum.tile([P, U], F32, name=f"level_turned{b}", tag="bank_b")
+            turn(level_turned, level[b][:, 0, :], every, True, True)
+            speed.append(keep.tile([P, 2, U], F32, name=f"speed{b}", tag=tag))
+            nc.scalar.activation(speed[b][:, 0, :], vel_turned[b][:], ACT.Abs)
+            nc.scalar.activation(speed[b][:, 1, :], vel[b][:, 1, :], ACT.Abs)
+            for side, source in enumerate((level_turned[:], level[b][:, 1, :])):
+                nc.scalar.activation(depth[b][:, side, :], source, ACT.Relu)
+                nc.scalar.activation(root[b][:, side, :], depth[b][:, side, :], ACT.Sqrt, scale=0.128, bias=0.0016)
+            wave_l.append(psum.tile([P, U], F32, name=f"wave_l{b}", tag=wave_tag))
+            turn(wave_l[b], speed[b][:, 0, :], every, True, False)
+            turn(wave_l[b], root[b][:, 0, :], every, False, True)
 
         halves = [slice(0, U // 2), slice(U // 2, U)]
+        chunks = [(0, 1), (2, 3)]
         for b in range(BLOCKS):
-            wave = keep.tile([P, 2, U], F32, name=f"wave{b}")
+            wave_r = keep.tile([P, U], F32, name=f"wave_r{b}")
             fastest = keep.tile([P, U], F32, name=f"fastest{b}")
-            shifted = keep.tile([P, 2, U], F32, name=f"shifted{b}")
+            shifted_r = keep.tile([P, U], F32, name=f"shifted_r{b}")
             flux = keep.tile([P, 2, U], F32, name=f"flux{b}")
             result = keep.tile([P, U], F32, name=f"result{b}")
-            for side in range(2):
-                nc.vector.tensor_tensor(wave[:, side, :], speed[b][:, side, :], root[b][:, side, :], ALU.add)
+            shifted_l = [psum.tile([P, U // 2], F32, name=f"shifted_l{b}{h}", tag=f"bank_s{h}") for h in range(2)]
+            flux_l = [psum.tile([P, U // 2], F32, name=f"flux_l{b}{h}", tag=f"bank_f{h}") for h in range(2)]
+            for h, c in enumerate(halves):
+                turn(shifted_l[h], vel[b][:, 0, :], chunks[h], True, False)
+                nc.vector.tensor_tensor(wave_r[:, c], speed[b][:, 1, c], root[b][:, 1, c], ALU.add)
+            for h, c in enumerate(halves):
+                nc.vector.tensor_tensor(fastest[:, c], wave_l[b][:, c], wave_r[:, c], ALU.max)
+                turn(shifted_l[h], fastest, chunks[h], False, True)
             for c in halves:
-                nc.vector.tensor_tensor(fastest[:, c], wave[:, 0, c], wave[:, 1, c], ALU.max)
+                nc.vector.tensor_tensor(shifted_r[:, c], vel[b][:, 1, c], fastest[:, c], ALU.subtract)
+            for h, c in enumerate(halves):
+                nc.vector.tensor_tensor(flux[:, 0, c], shifted_l[h][:], depth[b][:, 0, c], ALU.mult)
+                turn(flux_l[h], flux[:, 0, :], chunks[h], True, True)
             for c in halves:
-                nc.vector.tensor_tensor(shifted[:, 0, c], vel[b][:, 0, c], fastest[:, c], ALU.add)
-                nc.vector.tensor_tensor(shifted[:, 1, c], vel[b][:, 1, c], fastest[:, c], ALU.subtract)
-            for c in halves:
-                nc.vector.scalar_tensor_tensor(
-                    flux[:, :, c], depth[b][:, :, c], 0.5, shifted[:, :, c], ALU.mult, ALU.mult
-                )
-            for c in halves:
-                nc.vector.tensor_tensor(result[:, c], flux[:, 0, c], flux[:, 1, c], ALU.add)
+                nc.vector.tensor_tensor(flux[:, 1, c], shifted_r[:, c], depth[b][:, 1, c], ALU.mult)
+            for h, c in enumerate(halves):
+                nc.vector.tensor_tensor(result[:, c], flux_l[h][:], flux[:, 1, c], ALU.add)
                 nc.sync.dma_start(out[b * P : (b + 1) * P, c], result[:, c])

@@ -45,22 +45,19 @@ def tile_picked_yshwat_mass_p_kernel(
         nc.gpsimd.memset(scales[:].bitcast(I32), 0)
         identity = keep.tile([P, P], F32, name="identity")
         make_identity(nc, identity[:])
+        nc.sync.dma_start(bot_w[0][:, 0:S], bot[0:P, :])
         nc.sync.dma_start(rt_t[:], rt)
-        nc.sync.dma_start(
-            bot_w[0][:, 0 : BLOCKS * S].rearrange("p (b s) -> p b s", b=BLOCKS),
-            bot.rearrange("(b p) s -> p b s", p=P),
-        )
         nc.sync.dma_start(lf_t[:], lf)
         nc.sync.dma_start(raw_v[:], w2.rearrange("(p j) n -> p j n", j=PACK))
+        nc.sync.dma_start(words[:], x_words[0].rearrange("p n t -> p (n t)").bitcast(I32))
+        nc.sync.dma_start(offs_t[:], offs)
         for q in range(4):
             nc.sync.dma_start(
                 scales[32 * q : 32 * q + 4, :].bitcast(I32),
                 x_scales[0, 4 * q : 4 * q + 4, :].bitcast(I32),
             )
-        nc.sync.dma_start(offs_t[:], offs)
-        nc.sync.dma_start(words[:], x_words[0].rearrange("p n t -> p (n t)").bitcast(I32))
         nc.sync.dma_start(raw_h[:], w1.rearrange("(p j) n -> p j n", j=PACK))
-        nc.scalar.copy(bot_w[1][:, 0:S], bot_w[0][:, S : 2 * S])
+        nc.sync.dma_start(bot_w[1][:, 0:S], bot[P : 2 * P, :])
 
         grouped_v = keep.tile([P, N, PACK], BF16, name="grouped_v", align_bytes=64)
         grouped_h = keep.tile([P, N, PACK], BF16, name="grouped_h", align_bytes=64)
@@ -70,11 +67,14 @@ def tile_picked_yshwat_mass_p_kernel(
                 raw[:].rearrange("p t (c i) -> p c t i", i=4),
             )
 
-        bot_r = [keep.tile([P, U], F32, name=f"bot_r{b}") for b in range(BLOCKS)]
+        bot_r = [keep.tile([P, U], F32, name="bot_r0")]
         step0 = keep.tile([P, U], F32, name="step0")
-        nc.vector.tensor_copy(bot_r[0][:], bot_w[0][:].indirect(rt_t[:]))
-        nc.vector.tensor_tensor(step0[:], bot_w[0][:].indirect(lf_t[:]), bot_r[0][:], ALU.subtract)
-        nc.vector.tensor_copy(bot_r[1][:], bot_w[1][:].indirect(rt_t[:]))
+        halves = [slice(0, U // 2), slice(U // 2, U)]
+        list_halves = [slice(0, U // 32), slice(U // 32, U // 16)]
+        for c, entries in zip(halves, list_halves):
+            nc.vector.tensor_copy(bot_r[0][:, c], bot_w[0][:].indirect(rt_t[:, entries]))
+        for c, entries in zip(halves, list_halves):
+            nc.vector.tensor_tensor(step0[:, c], bot_w[0][:].indirect(lf_t[:, entries]), bot_r[0][:, c], ALU.subtract)
 
         x_codes = keep.tile([P, S], U32, name="x_codes", align_bytes=64)
         x_sc = keep.tile([P, S], U8, name="x_sc", align_bytes=64)
@@ -102,11 +102,13 @@ def tile_picked_yshwat_mass_p_kernel(
             return acc
 
         yv = product(grouped_v, "yv")
+        bot_r.append(keep.tile([P, U], F32, name="bot_r1", tag="scales"))
+        nc.vector.tensor_copy(bot_r[1][:], bot_w[1][:].indirect(rt_t[:]))
         yh = product(grouped_h, "yh")
 
-        late = keep.tile([P, 5, U], F32, name="late", tag="grouped_h", align_bytes=64)
-        step = [step0[:], late[:, 4, :]]
-        vel = [late[:, 0:2, :], late[:, 2:4, :]]
+        late = keep.tile([P, 4, U], F32, name="late", tag="grouped_h", align_bytes=64)
+        step = [step0[:], late[:, 3, :]]
+        vel = [[late[:, 0, :], late[:, 1, :]], [late[:, 2, :]]]
         nc.vector.tensor_tensor(step[1], bot_w[1][:].indirect(lf_t[:]), bot_r[1][:], ALU.subtract)
 
         def cut_depths(b, tag):
@@ -141,14 +143,17 @@ def tile_picked_yshwat_mass_p_kernel(
                 )
 
         every = range(U // P)
+
+        def fetch_velocity(b, side):
+            nc.vector.tensor_copy(vel[b][side], vel_w[:, b * S : b * S + COPY_WINDOW].indirect(sides[side][:]))
+
         vel_turned = []
         for b, tag in enumerate(("bank_a", "yv")):
-            for side in range(2):
-                nc.vector.tensor_copy(
-                    vel[b][:, side, :], vel_w[:, b * S : b * S + COPY_WINDOW].indirect(sides[side][:])
-                )
+            fetch_velocity(b, 0)
             vel_turned.append(psum.tile([P, U], F32, name=f"vel_turned{b}", tag=tag))
-            turn(vel_turned[b], vel[b][:, 0, :], every, True, True)
+            turn(vel_turned[b], vel[b][0], every, True, True)
+            if b == 0:
+                fetch_velocity(0, 1)
         for b in range(BLOCKS):
             nc.vector.scalar_tensor_tensor(soft_w[b][:, 0:S], yh[:, b, :], 0.0, tail[:, b, :], ALU.max, ALU.add)
 
@@ -162,11 +167,14 @@ def tile_picked_yshwat_mass_p_kernel(
                 nc.vector.tensor_tensor(
                     level[b][:, side, :], soft_w[b][:].indirect(sides[side][:]), cut[b][:, side, :], ALU.subtract
                 )
+            if b == 0:
+                vel[1].append(keep.tile([P, U], F32, name="vel_last", tag="tail")[:])
+                fetch_velocity(1, 1)
             level_turned = psum.tile([P, U], F32, name=f"level_turned{b}", tag="bank_b")
             turn(level_turned, level[b][:, 0, :], every, True, True)
             speed.append(keep.tile([P, 2, U], F32, name=f"speed{b}", tag=tag))
             nc.scalar.activation(speed[b][:, 0, :], vel_turned[b][:], ACT.Abs)
-            nc.scalar.activation(speed[b][:, 1, :], vel[b][:, 1, :], ACT.Abs)
+            nc.scalar.activation(speed[b][:, 1, :], vel[b][1], ACT.Abs)
             for side, source in enumerate((level_turned[:], level[b][:, 1, :])):
                 nc.scalar.activation(depth[b][:, side, :], source, ACT.Relu)
                 nc.scalar.activation(root[b][:, side, :], depth[b][:, side, :], ACT.Sqrt, scale=0.128, bias=0.0016)
@@ -174,7 +182,6 @@ def tile_picked_yshwat_mass_p_kernel(
             turn(wave_l[b], speed[b][:, 0, :], every, True, False)
             turn(wave_l[b], root[b][:, 0, :], every, False, True)
 
-        halves = [slice(0, U // 2), slice(U // 2, U)]
         chunks = [(0, 1), (2, 3)]
         for b in range(BLOCKS):
             wave_r = keep.tile([P, U], F32, name=f"wave_r{b}")
@@ -185,13 +192,13 @@ def tile_picked_yshwat_mass_p_kernel(
             shifted_l = [psum.tile([P, U // 2], F32, name=f"shifted_l{b}{h}", tag=f"bank_s{h}") for h in range(2)]
             flux_l = [psum.tile([P, U // 2], F32, name=f"flux_l{b}{h}", tag=f"bank_f{h}") for h in range(2)]
             for h, c in enumerate(halves):
-                turn(shifted_l[h], vel[b][:, 0, :], chunks[h], True, False)
+                turn(shifted_l[h], vel[b][0], chunks[h], True, False)
                 nc.vector.tensor_tensor(wave_r[:, c], speed[b][:, 1, c], root[b][:, 1, c], ALU.add)
             for h, c in enumerate(halves):
                 nc.vector.tensor_tensor(fastest[:, c], wave_l[b][:, c], wave_r[:, c], ALU.max)
                 turn(shifted_l[h], fastest, chunks[h], False, True)
             for c in halves:
-                nc.vector.tensor_tensor(shifted_r[:, c], vel[b][:, 1, c], fastest[:, c], ALU.subtract)
+                nc.vector.tensor_tensor(shifted_r[:, c], vel[b][1][:, c], fastest[:, c], ALU.subtract)
             for h, c in enumerate(halves):
                 nc.vector.tensor_tensor(flux[:, 0, c], shifted_l[h][:], depth[b][:, 0, c], ALU.mult)
                 turn(flux_l[h], flux[:, 0, :], chunks[h], True, True)

@@ -42,12 +42,13 @@ def tile_picked_yshwat_mass_p_kernel(
         raw_h = keep.tile([P, PACK, N], F32, name="raw_h")
         raw_v = keep.tile([P, PACK, N], F32, name="raw_v")
 
-        nc.gpsimd.memset(scales[:].bitcast(I32), 0)
+        nc.vector.memset(scales[:].bitcast(I32), 0)
         identity = keep.tile([P, P], F32, name="identity")
         make_identity(nc, identity[:])
         nc.sync.dma_start(bot_w[0][:, 0:S], bot[0:P, :])
         nc.sync.dma_start(rt_t[:], rt)
         nc.sync.dma_start(lf_t[:], lf)
+        nc.sync.dma_start(bot_w[1][:, 0:S], bot[P : 2 * P, :])
         nc.sync.dma_start(raw_v[:], w2.rearrange("(p j) n -> p j n", j=PACK))
         nc.sync.dma_start(words[:], x_words[0].rearrange("p n t -> p (n t)").bitcast(I32))
         nc.sync.dma_start(offs_t[:], offs)
@@ -57,7 +58,6 @@ def tile_picked_yshwat_mass_p_kernel(
                 x_scales[0, 4 * q : 4 * q + 4, :].bitcast(I32),
             )
         nc.sync.dma_start(raw_h[:], w1.rearrange("(p j) n -> p j n", j=PACK))
-        nc.sync.dma_start(bot_w[1][:, 0:S], bot[P : 2 * P, :])
 
         grouped_v = keep.tile([P, N, PACK], BF16, name="grouped_v", align_bytes=64)
         grouped_h = keep.tile([P, N, PACK], BF16, name="grouped_h", align_bytes=64)
@@ -67,7 +67,7 @@ def tile_picked_yshwat_mass_p_kernel(
                 raw[:].rearrange("p t (c i) -> p c t i", i=4),
             )
 
-        bot_r = [keep.tile([P, U], F32, name="bot_r0")]
+        bot_r = [keep.tile([P, U], F32, name=f"bot_r{b}") for b in range(BLOCKS)]
         step0 = keep.tile([P, U], F32, name="step0")
         halves = [slice(0, U // 2), slice(U // 2, U)]
         list_halves = [slice(0, U // 32), slice(U // 32, U // 16)]
@@ -75,6 +75,7 @@ def tile_picked_yshwat_mass_p_kernel(
             nc.vector.tensor_copy(bot_r[0][:, c], bot_w[0][:].indirect(rt_t[:, entries]))
         for c, entries in zip(halves, list_halves):
             nc.vector.tensor_tensor(step0[:, c], bot_w[0][:].indirect(lf_t[:, entries]), bot_r[0][:, c], ALU.subtract)
+        nc.vector.tensor_copy(bot_r[1][:], bot_w[1][:].indirect(rt_t[:]))
 
         x_codes = keep.tile([P, S], U32, name="x_codes", align_bytes=64)
         x_sc = keep.tile([P, S], U8, name="x_sc", align_bytes=64)
@@ -102,8 +103,6 @@ def tile_picked_yshwat_mass_p_kernel(
             return acc
 
         yv = product(grouped_v, "yv")
-        bot_r.append(keep.tile([P, U], F32, name="bot_r1", tag="scales"))
-        nc.vector.tensor_copy(bot_r[1][:], bot_w[1][:].indirect(rt_t[:]))
         yh = product(grouped_h, "yh")
 
         late = keep.tile([P, 4, U], F32, name="late", tag="grouped_h", align_bytes=64)

from contextlib import ExitStack

import concourse.mybir as mybir
from concourse.masks import make_identity

K, T, S, N, U = 512, 1024, 256, 256, 512
FLOPS = 2 * 2 * K * N * S

F32 = mybir.dt.float32
BF16 = mybir.dt.bfloat16
I32 = mybir.dt.int32
U32 = mybir.dt.uint32
U16 = mybir.dt.uint16
U8 = mybir.dt.uint8
FP8X4 = mybir.dt.float8_e4m3fn_x4
ACT = mybir.ActivationFunctionType
ALU = mybir.AluOpType

P = 128
PACK = 4
BLOCKS = N // P
WIDE = 2 * U
COPY_WINDOW = 704


def tile_picked_yshwat_mass_p_kernel(
    tc, x_words, x_scales, w1, w2, bot, offs, lf, rt, out
):
    nc = tc.nc
    with ExitStack() as ctx:
        keep = ctx.enter_context(tc.tile_pool(name="keep", bufs=1))
        psum = ctx.enter_context(tc.psum_pool(name="psum", bufs=1))

        offs_t = keep.tile([P, S // 16], U16, name="offs_t")
        lf_t = keep.tile([P, U // 16], U16, name="lf_t")
        rt_t = keep.tile([P, U // 16], U16, name="rt_t")
        sides = (lf_t, rt_t)
        words = keep.tile([P, T], I32, name="words")
        scales = keep.tile([P, T], U8, name="scales")
        bot_w = [keep.tile([P, WIDE], F32, name=f"bot_w{b}") for b in range(BLOCKS)]
        soft_w = [keep.tile([P, WIDE], F32, name=f"soft_w{b}") for b in range(BLOCKS)]
        raw_h = keep.tile([P, PACK, N], F32, name="raw_h")
        raw_v = keep.tile([P, PACK, N], F32, name="raw_v")

        nc.vector.memset(scales[:].bitcast(I32), 0)
        identity = keep.tile([P, P], F32, name="identity")
        make_identity(nc, identity[:])
        nc.sync.dma_start(bot_w[0][:, 0:S], bot[0:P, :])
        nc.sync.dma_start(rt_t[:], rt)
        nc.sync.dma_start(lf_t[:], lf)
        nc.sync.dma_start(bot_w[1][:, 0:S], bot[P : 2 * P, :])
        nc.sync.dma_start(raw_v[:], w2.rearrange("(p j) n -> p j n", j=PACK))
        nc.sync.dma_start(words[:], x_words[0].rearrange("p n t -> p (n t)").bitcast(I32))
        nc.sync.dma_start(offs_t[:], offs)
        for q in range(4):
            nc.sync.dma_start(
                scales[32 * q : 32 * q + 4, :].bitcast(I32),
                x_scales[0, 4 * q : 4 * q + 4, :].bitcast(I32),
            )
        nc.sync.dma_start(raw_h[:], w1.rearrange("(p j) n -> p j n", j=PACK))

        grouped_v = keep.tile([P, N, PACK], BF16, name="grouped_v", align_bytes=64)
        grouped_h = keep.tile([P, N, PACK], BF16, name="grouped_h", align_bytes=64)
        for grouped, raw in ((grouped_v, raw_v), (grouped_h, raw_h)):
            nc.scalar.copy(
                grouped[:].rearrange("p (c i) t -> p c t i", i=4),
                raw[:].rearrange("p t (c i) -> p c t i", i=4),
            )

        bot_r = [keep.tile([P, U], F32, name=f"bot_r{b}") for b in range(BLOCKS)]
        step0 = keep.tile([P, U], F32, name="step0")
        halves = [slice(0, U // 2), slice(U // 2, U)]
        list_halves = [slice(0, U // 32), slice(U // 32, U // 16)]
        for c, entries in zip(halves, list_halves):
            nc.vector.tensor_copy(bot_r[0][:, c], bot_w[0][:].indirect(rt_t[:, entries]))
        for c, entries in zip(halves, list_halves):
            nc.vector.tensor_tensor(step0[:, c], bot_w[0][:].indirect(lf_t[:, entries]), bot_r[0][:, c], ALU.subtract)
        nc.vector.tensor_copy(bot_r[1][:], bot_w[1][:].indirect(rt_t[:]))

        x_codes = keep.tile([P, S], U32, name="x_codes", align_bytes=64)
        x_sc = keep.tile([P, S], U8, name="x_sc", align_bytes=64)
        nc.vector.tensor_copy(x_codes[:], words[:].bitcast(U32).indirect(offs_t[:]))
        nc.vector.tensor_copy(x_sc[:], scales[:].indirect(offs_t[:]))

        def product(grouped, name):
            codes = keep.tile([P, N], U32, name=name + "_codes", align_bytes=64)
            plane = keep.tile([P, N], U8, name=name + "_plane", align_bytes=64)
            acc = psum.tile([P, BLOCKS, S], F32, name=name)
            nc.vector.quantize_mx(
                out=codes[:].bitcast(FP8X4), scales=plane[:], in_=grouped[:].rearrange("p n t -> p (n t)")
            )
            for b in range(BLOCKS):
                cols = slice(b * P, (b + 1) * P)
                nc.tensor.matmul_mx(
                    out=acc[:, b, :],
                    lhsT=codes[:, cols].bitcast(FP8X4),
                    lhsT_scale=plane[:, cols],
                    rhs=x_codes[:].bitcast(FP8X4),
                    rhs_scale=x_sc[:],
                    start=True,
                    stop=True,
                )
            return acc

        yv = product(grouped_v, "yv")
        yh = product(grouped_h, "yh")

        late = keep.tile([P, 4, U], F32, name="late", tag="grouped_h", align_bytes=64)
        step = [step0[:], late[:, 3, :]]
        vel = [[late[:, 0, :], late[:, 1, :]], [late[:, 2, :]]]
        nc.vector.tensor_tensor(step[1], bot_w[1][:].indirect(lf_t[:]), bot_r[1][:], ALU.subtract)

        def cut_depths(b, tag):
            cut = keep.tile([P, 2, U], F32, name=f"cut{b}", tag=tag)
            nc.scalar.activation(cut[:, 0, :], step[b], ACT.Relu, scale=-1.25)
            nc.scalar.activation(cut[:, 1, :], step[b], ACT.Relu, scale=1.25)
            return cut

        cut = [cut_depths(0, "raw_v")]
        vel_w = keep.tile([P, S + COPY_WINDOW], F32, name="vel_w", tag="raw_h")
        for b in range(BLOCKS):
            nc.scalar.activation(vel_w[:, b * S : (b + 1) * S], yv[:, b, :], ACT.Copy, scale=0.4)
        size = keep.tile([P, BLOCKS * S], F32, name="size")
        decay = keep.tile([P, BLOCKS * S], F32, name="decay")
        tail = keep.tile([P, BLOCKS, S], F32, name="tail")
        nc.scalar.activation(size[:], yh[:].rearrange("p b s -> p (b s)"), ACT.Abs)
        nc.scalar.activation(decay[:], size[:], ACT.Exp, scale=-1.0)
        nc.scalar.activation(tail[:].rearrange("p b s -> p (b s)"), decay[:], ACT.Ln, bias=1.0)
        warm = keep.tile([P, 1], F32, name="warm")
        nc.scalar.activation(warm[:], tail[:, 0, 0:1], ACT.Sqrt, bias=1.0)
        cut.append(cut_depths(1, "size"))

        def turn(bank, tile, chunks, start, stop):
            for n, c in enumerate(chunks):
                nc.tensor.matmul(
                    bank[:, n * P : (n + 1) * P],
                    tile[:, c * P : (c + 1) * P],
                    identity[:],
                    start=start and n == 0,
                    stop=stop and n == len(chunks) - 1,
                    is_transpose=True,
                )

        every = range(U // P)

        def fetch_velocity(b, side):
            nc.vector.tensor_copy(vel[b][side], vel_w[:, b * S : b * S + COPY_WINDOW].indirect(sides[side][:]))

        vel_turned = []
        for b, tag in enumerate(("bank_a", "yv")):
            fetch_velocity(b, 0)
            vel_turned.append(psum.tile([P, U], F32, name=f"vel_turned{b}", tag=tag))
            turn(vel_turned[b], vel[b][0], every, True, True)
            if b == 0:
                fetch_velocity(0, 1)
        for b in range(BLOCKS):
            nc.vector.scalar_tensor_tensor(soft_w[b][:, 0:S], yh[:, b, :], 0.0, tail[:, b, :], ALU.max, ALU.add)

        level = [keep.tile([P, 2, U], F32, name=f"level{b}") for b in range(BLOCKS)]
        depth = [keep.tile([P, 2, U], F32, name=f"depth{b}") for b in range(BLOCKS)]
        root = [keep.tile([P, 2, U], F32, name=f"root{b}") for b in range(BLOCKS)]
        speed = []
        wave_l = []
        for b, (tag, wave_tag) in enumerate((("decay", "bank_a"), ("level0", "yh"))):
            for side in range(2):
                nc.vector.tensor_tensor(
                    level[b][:, side, :], soft_w[b][:].indirect(sides[side][:]), cut[b][:, side, :], ALU.subtract
                )
            if b == 0:
                vel[1].append(keep.tile([P, U], F32, name="vel_last", tag="tail")[:])
                fetch_velocity(1, 1)
            level_turned = psum.tile([P, U], F32, name=f"level_turned{b}", tag="bank_b")
            turn(level_turned, level[b][:, 0, :], every, True, True)
            speed.append(keep.tile([P, 2, U], F32, name=f"speed{b}", tag=tag))
            nc.scalar.activation(speed[b][:, 0, :], vel_turned[b][:], ACT.Abs)
            nc.scalar.activation(speed[b][:, 1, :], vel[b][1], ACT.Abs)
            for side, source in enumerate((level_turned[:], level[b][:, 1, :])):
                nc.scalar.activation(depth[b][:, side, :], source, ACT.Relu)
                nc.scalar.activation(root[b][:, side, :], depth[b][:, side, :], ACT.Sqrt, scale=0.128, bias=0.0016)
            wave_l.append(psum.tile([P, U], F32, name=f"wave_l{b}", tag=wave_tag))
            turn(wave_l[b], speed[b][:, 0, :], every, True, False)
            turn(wave_l[b], root[b][:, 0, :], every, False, True)

        chunks = [(0, 1), (2, 3)]
        for b in range(BLOCKS):
            wave_r = keep.tile([P, U], F32, name=f"wave_r{b}")
            fastest = keep.tile([P, U], F32, name=f"fastest{b}")
            shifted_r = keep.tile([P, U], F32, name=f"shifted_r{b}")
            flux = keep.tile([P, 2, U], F32, name=f"flux{b}")
            result = keep.tile([P, U], F32, name=f"result{b}")
            shifted_l = [psum.tile([P, U // 2], F32, name=f"shifted_l{b}{h}", tag=f"bank_s{h}") for h in range(2)]
            flux_l = [psum.tile([P, U // 2], F32, name=f"flux_l{b}{h}", tag=f"bank_f{h}") for h in range(2)]
            for h, c in enumerate(halves):
                turn(shifted_l[h], vel[b][0], chunks[h], True, False)
                nc.vector.tensor_tensor(wave_r[:, c], speed[b][:, 1, c], root[b][:, 1, c], ALU.add)
            for h, c in enumerate(halves):
                nc.vector.tensor_tensor(fastest[:, c], wave_l[b][:, c], wave_r[:, c], ALU.max)
                turn(shifted_l[h], fastest, chunks[h], False, True)
            for c in halves:
                nc.vector.tensor_tensor(shifted_r[:, c], vel[b][1][:, c], fastest[:, c], ALU.subtract)
            for h, c in enumerate(halves):
                nc.vector.tensor_tensor(flux[:, 0, c], shifted_l[h][:], depth[b][:, 0, c], ALU.mult)
                turn(flux_l[h], flux[:, 0, :], chunks[h], True, True)
            for c in halves:
                nc.vector.tensor_tensor(flux[:, 1, c], shifted_r[:, c], depth[b][:, 1, c], ALU.mult)
            for h, c in enumerate(halves):
                nc.vector.tensor_tensor(result[:, c], flux_l[h][:], flux[:, 1, c], ALU.add)
                nc.sync.dma_start(out[b * P : (b + 1) * P, c], result[:, c])
